import numpy as np
import ml_dtypes

BF16 = ml_dtypes.bfloat16


def bf(x):
    return np.asarray(x, np.float32).astype(BF16)


def f32(x):
    return np.asarray(x, np.float32)


def f64(x):
    return np.asarray(x).astype(np.float64)


def striped(idx):
    return np.tile(idx.reshape(-1, 16).T, (8, 1))


S, K, M, N, B, Q = 512, 128, 256, 384, 2, 192


def setup_inputs():
    return {"base": bf(np.random.standard_normal((B, M, S))), "x": bf(np.random.standard_normal((K, N))), "w": bf(np.random.standard_normal((K, M)) / np.sqrt(K)), "b": f32(0.5 * np.random.standard_normal((M, 1))), "offs": striped(np.random.permutation(S)[:N])}


def reference(base, x, w, b, offs):
    idx = offs[:16].T.reshape(-1)
    z = f64(base).copy()
    for i in range(B):
        z[i][:, idx[i * Q : (i + 1) * Q]] = f64(w).T @ f64(x)[:, i * Q : (i + 1) * Q]
    return np.tanh(z + f64(b))

@@ -1,0 +1,59 @@
+import concourse.mybir as mybir
+from concourse.masks import make_identity
+
+P = 128
+SEQS, FEATS, TOKENS = 2, 256, 512
+ENTRIES = 384
+PIECE = ENTRIES // SEQS
+PIECE_COLUMNS = PIECE // 16
+
+BF16, F32, U16 = mybir.dt.bfloat16, mybir.dt.float32, mybir.dt.uint16
+TANH = mybir.ActivationFunctionType.Tanh
+
+FLOPS = 2 * P * FEATS * ENTRIES
+
+
+def tile_scatter_matmul_kernel(tc, base, x, w, b, offs, out):
+    nc = tc.nc
+    blocks = FEATS // P
+    windows = [(i, a) for i in range(SEQS) for a in range(blocks)]
+
+    with (
+        tc.tile_pool(name="held", bufs=1) as held,
+        tc.psum_pool(name="psum", bufs=1) as psum,
+    ):
+        base_tiles = {}
+        for i, a in windows:
+            base_tiles[i, a] = held.tile([P, TOKENS], BF16, name=f"base_{i}_{a}")
+            nc.sync.dma_start(base_tiles[i, a][:], base[i, a * P : (a + 1) * P, :])
+        weights = held.tile([P, FEATS], BF16, name="weights")
+        nc.sync.dma_start(weights[:], w)
+        moving = held.tile([P, ENTRIES], BF16, name="moving")
+        nc.sync.dma_start(moving[:], x)
+        offsets = held.tile([P, ENTRIES // 16], U16, name="offsets")
+        nc.sync.dma_start(offsets[:], offs)
+        bias = held.tile([P, blocks], F32, name="bias")
+        nc.scalar.dma_start(bias[:], b.rearrange("(a p) o -> p (a o)", p=P))
+
+        identity = held.tile([P, P], BF16, name="identity")
+        make_identity(nc, identity[:])
+
+        window_tiles = {}
+        for i, a in windows:
+            window_tiles[i, a] = psum.tile([P, TOKENS], F32, name=f"window_{i}_{a}")
+            nc.tensor.matmul(window_tiles[i, a][:], identity[:], base_tiles[i, a][:], start=True, stop=True)
+
+        for i, a in windows:
+            piece = offsets[:, i * PIECE_COLUMNS : (i + 1) * PIECE_COLUMNS]
+            nc.tensor.matmul(
+                window_tiles[i, a][:].indirect(piece),
+                weights[:, a * P : (a + 1) * P],
+                moving[:, i * PIECE : (i + 1) * PIECE],
+                start=True,
+                stop=True,
+            )
+
+        for i, a in windows:
+            result = held.tile([P, TOKENS], F32, name=f"result_{i}_{a}")
+            nc.scalar.activation(result[:], window_tiles[i, a][:], TANH, bias=bias[:, a : a + 1])
+            nc.sync.dma_start(out[i, a * P : (a + 1) * P, :], result[:])

@@ -6,6 +6,7 @@ SEQS, FEATS, TOKENS = 2, 256, 512
 ENTRIES = 384
 PIECE = ENTRIES // SEQS
 PIECE_COLUMNS = PIECE // 16
+WARM_UPS = 3
 
 BF16, F32, U16 = mybir.dt.bfloat16, mybir.dt.float32, mybir.dt.uint16
 TANH = mybir.ActivationFunctionType.Tanh
@@ -37,6 +38,14 @@ def tile_scatter_matmul_kernel(tc, base, x, w, b, offs, out):
 
         identity = held.tile([P, P], BF16, name="identity")
         make_identity(nc, identity[:])
+
+        zeros = held.tile([P, TOKENS], BF16, name="zeros")
+        nc.vector.memset(zeros[:], 0.0)
+        tanh_of_zero = held.tile([P, 1], F32, name="tanh_of_zero")
+        nc.scalar.activation(tanh_of_zero[:], zeros[:, :1], TANH)
+        spare = psum.tile([P, TOKENS], F32, name="spare")
+        for turn in range(WARM_UPS):
+            nc.tensor.matmul(spare[:], zeros[:, :P], zeros[:], start=True, stop=True)
 
         window_tiles = {}
         for i, a in windows:

@@ -6,7 +6,8 @@ SEQS, FEATS, TOKENS = 2, 256, 512
 ENTRIES = 384
 PIECE = ENTRIES // SEQS
 PIECE_COLUMNS = PIECE // 16
-WARM_UPS = 3
+FIRST_CUTS, LATER_CUTS = 1, 16
+WARM_UPS = 2
 
 BF16, F32, U16 = mybir.dt.bfloat16, mybir.dt.float32, mybir.dt.uint16
 TANH = mybir.ActivationFunctionType.Tanh
@@ -24,15 +25,20 @@ def tile_scatter_matmul_kernel(tc, base, x, w, b, offs, out):
         tc.psum_pool(name="psum", bufs=1) as psum,
     ):
         base_tiles = {}
-        for i, a in windows:
-            base_tiles[i, a] = held.tile([P, TOKENS], BF16, name=f"base_{i}_{a}")
-            nc.sync.dma_start(base_tiles[i, a][:], base[i, a * P : (a + 1) * P, :])
+
+        def load_base(i):
+            for a in range(blocks):
+                base_tiles[i, a] = held.tile([P, TOKENS], BF16, name=f"base_{i}_{a}")
+                nc.sync.dma_start(base_tiles[i, a][:], base[i, a * P : (a + 1) * P, :])
+
+        load_base(0)
         weights = held.tile([P, FEATS], BF16, name="weights")
         nc.sync.dma_start(weights[:], w)
         moving = held.tile([P, ENTRIES], BF16, name="moving")
         nc.sync.dma_start(moving[:], x)
         offsets = held.tile([P, ENTRIES // 16], U16, name="offsets")
         nc.sync.dma_start(offsets[:], offs)
+        load_base(1)
         bias = held.tile([P, blocks], F32, name="bias")
         nc.scalar.dma_start(bias[:], b.rearrange("(a p) o -> p (a o)", p=P))
 
@@ -48,19 +54,27 @@ def tile_scatter_matmul_kernel(tc, base, x, w, b, offs, out):
             nc.tensor.matmul(spare[:], zeros[:, :P], zeros[:], start=True, stop=True)
 
         window_tiles = {}
-        for i, a in windows:
-            window_tiles[i, a] = psum.tile([P, TOKENS], F32, name=f"window_{i}_{a}")
-            nc.tensor.matmul(window_tiles[i, a][:], identity[:], base_tiles[i, a][:], start=True, stop=True)
-
-        for i, a in windows:
+        for i in range(SEQS):
+            step = TOKENS // (FIRST_CUTS if i == 0 else LATER_CUTS)
+            for a in range(blocks):
+                window_tiles[i, a] = psum.tile([P, TOKENS], F32, name=f"window_{i}_{a}")
+                for t in range(0, TOKENS, step):
+                    nc.tensor.matmul(
+                        window_tiles[i, a][:, t : t + step],
+                        identity[:],
+                        base_tiles[i, a][:, t : t + step],
+                        start=True,
+                        stop=True,
+                    )
             piece = offsets[:, i * PIECE_COLUMNS : (i + 1) * PIECE_COLUMNS]
-            nc.tensor.matmul(
-                window_tiles[i, a][:].indirect(piece),
-                weights[:, a * P : (a + 1) * P],
-                moving[:, i * PIECE : (i + 1) * PIECE],
-                start=True,
-                stop=True,
-            )
+            for a in range(blocks):
+                nc.tensor.matmul(
+                    window_tiles[i, a][:].indirect(piece),
+                    weights[:, a * P : (a + 1) * P],
+                    moving[:, i * PIECE : (i + 1) * PIECE],
+                    start=True,
+                    stop=True,
+                )
 
         for i, a in windows:
             result = held.tile([P, TOKENS], F32, name=f"result_{i}_{a}")

import concourse.mybir as mybir
from concourse.masks import make_identity

P = 128
SEQS, FEATS, TOKENS = 2, 256, 512
ENTRIES = 384
PIECE = ENTRIES // SEQS
PIECE_COLUMNS = PIECE // 16
FIRST_CUTS, LATER_CUTS = 1, 16
WARM_UPS = 2

BF16, F32, U16 = mybir.dt.bfloat16, mybir.dt.float32, mybir.dt.uint16
TANH = mybir.ActivationFunctionType.Tanh

FLOPS = 2 * P * FEATS * ENTRIES


def tile_scatter_matmul_kernel(tc, base, x, w, b, offs, out):
    nc = tc.nc
    blocks = FEATS // P
    windows = [(i, a) for i in range(SEQS) for a in range(blocks)]

    with (
        tc.tile_pool(name="held", bufs=1) as held,
        tc.psum_pool(name="psum", bufs=1) as psum,
    ):
        base_tiles = {}

        def load_base(i):
            for a in range(blocks):
                base_tiles[i, a] = held.tile([P, TOKENS], BF16, name=f"base_{i}_{a}")
                nc.sync.dma_start(base_tiles[i, a][:], base[i, a * P : (a + 1) * P, :])

        load_base(0)
        weights = held.tile([P, FEATS], BF16, name="weights")
        nc.sync.dma_start(weights[:], w)
        moving = held.tile([P, ENTRIES], BF16, name="moving")
        nc.sync.dma_start(moving[:], x)
        offsets = held.tile([P, ENTRIES // 16], U16, name="offsets")
        nc.sync.dma_start(offsets[:], offs)
        load_base(1)
        bias = held.tile([P, blocks], F32, name="bias")
        nc.scalar.dma_start(bias[:], b.rearrange("(a p) o -> p (a o)", p=P))

        identity = held.tile([P, P], BF16, name="identity")
        make_identity(nc, identity[:])

        zeros = held.tile([P, TOKENS], BF16, name="zeros")
        nc.vector.memset(zeros[:], 0.0)
        tanh_of_zero = held.tile([P, 1], F32, name="tanh_of_zero")
        nc.scalar.activation(tanh_of_zero[:], zeros[:, :1], TANH)
        spare = psum.tile([P, TOKENS], F32, name="spare")
        for turn in range(WARM_UPS):
            nc.tensor.matmul(spare[:], zeros[:, :P], zeros[:], start=True, stop=True)

        window_tiles = {}
        for i in range(SEQS):
            step = TOKENS // (FIRST_CUTS if i == 0 else LATER_CUTS)
            for a in range(blocks):
                window_tiles[i, a] = psum.tile([P, TOKENS], F32, name=f"window_{i}_{a}")
                for t in range(0, TOKENS, step):
                    nc.tensor.matmul(
                        window_tiles[i, a][:, t : t + step],
                        identity[:],
                        base_tiles[i, a][:, t : t + step],
                        start=True,
                        stop=True,
                    )
            piece = offsets[:, i * PIECE_COLUMNS : (i + 1) * PIECE_COLUMNS]
            for a in range(blocks):
                nc.tensor.matmul(
                    window_tiles[i, a][:].indirect(piece),
                    weights[:, a * P : (a + 1) * P],
                    moving[:, i * PIECE : (i + 1) * PIECE],
                    start=True,
                    stop=True,
                )

        for i, a in windows:
            result = held.tile([P, TOKENS], F32, name=f"result_{i}_{a}")
            nc.scalar.activation(result[:], window_tiles[i, a][:], TANH, bias=bias[:, a : a + 1])
            nc.sync.dma_start(out[i, a * P : (a + 1) * P, :], result[:])
